import numpy as np
import ml_dtypes


def mxq(x, axis, fmt="e4m3"):
    dtype, down = {"e4m3": (ml_dtypes.float8_e4m3fn, 7), "e5m2": (ml_dtypes.float8_e5m2, 14)}[fmt]
    v = np.moveaxis(np.asarray(x, np.float32).astype(ml_dtypes.bfloat16).astype(np.float64), axis, -1)
    blocks = v.reshape(v.shape[:-1] + (-1, 32))
    amax = np.abs(blocks).max(-1, keepdims=True)
    byte = np.maximum(np.where(amax > 0, np.frexp(amax)[1] - 1 + 127, 0) - down, 1)
    scale = np.exp2(byte - 127.0)
    codes = (blocks / scale).astype(np.float32).astype(dtype).astype(np.float64)
    return np.moveaxis((codes * scale).reshape(v.shape), -1, axis)


WIDE = False


def mx_kscale(k):
    if not WIDE:
        return np.ones(k)
    levels = np.array([10, -10, 5, -5, 0])
    if k % 512:
        return np.exp2(np.random.permutation(np.resize(levels, k // 32))).repeat(32)
    a = np.empty((k // 512, 16))
    for p in range(k // 512):
        a[p, :8] = np.random.permutation(np.resize(levels, 8))
        for g in range(8):
            far = levels[np.abs(levels - a[p, g]) >= 10]
            a[p, g + 8] = far[np.random.randint(len(far))]
    return np.exp2(a.ravel()).repeat(32)


def f64(x):
    return np.asarray(x).astype(np.float64)


def striped8(idx):
    return np.concatenate([x.reshape(-1, 16).T for x in idx]).astype(np.uint16)


def runs(offs, k):
    lists = np.stack([offs[16 * r : 16 * r + 16].T.reshape(-1) for r in range(8)]).astype(np.int64)
    return lists[np.arange(k) % 512 // 64]


def pack_weight(w):
    k, n = w.shape
    w = f64(np.asarray(w, np.float32).astype(ml_dtypes.bfloat16)).reshape(k // 32, 32, n)
    amax = np.abs(w).max(1)
    byte = np.clip(np.where(amax > 0, np.frexp(amax)[1] - 1 + 127 - 7, 1), 1, 254)
    scaled = (w * np.exp2(127.0 - byte)[:, None, :]).reshape(k, n).astype(np.float32)
    words = np.ascontiguousarray(scaled.reshape(k // 512, 128, 4, n).transpose(0, 1, 3, 2)).astype(ml_dtypes.float8_e4m3fn).view(np.uint8)
    return words, np.ascontiguousarray(byte.astype(np.uint8).reshape(k // 512, 16, n))


def unpack_weight(words, scales):
    g, p, n, _ = words.shape
    vals = np.ascontiguousarray(words).view(ml_dtypes.float8_e4m3fn).astype(np.float64) * np.repeat(np.exp2(scales.astype(np.float64) - 127.0), 8, axis=1)[..., None]
    return vals.transpose(0, 1, 3, 2).reshape(g * 512, n)


K, T, S, N, H = 512, 2048, 512, 512, 512


def setup_inputs():
    n = np.random.standard_normal
    s = mx_kscale(K)[:, None]
    u = mx_kscale(H)
    packed_xT = pack_weight(n((K, T)) * s)
    return {
        "x_words": packed_xT[0],
        "x_scales": packed_xT[1],
        "w1": (n((K, H)) / np.sqrt(K) / s).astype(np.float32),
        "gn": (np.random.uniform(0.5, 1.5, (H, 1)) * u[:, None]).astype(np.float32),
        "w2": (n((H, N)) / np.sqrt(H) / u[:, None]).astype(np.float32),
        "offs": striped8(np.random.randint(0, T, (8, S))),
        "n1": striped8(np.stack([np.random.permutation(S) for _ in range(8)])),
        "n2": striped8(np.stack([np.random.permutation(S) for _ in range(8)])),
        "n3": striped8(np.stack([np.random.permutation(S) for _ in range(8)])),
    }


def reference(x_words, x_scales, w1, gn, w2, offs, n1, n2, n3):
    xq = unpack_weight(x_words, x_scales)[np.arange(K)[:, None], runs(offs, K)]
    y = mxq(f64(w1), 0, "e4m3").T @ xq
    z = f64(gn) * (y[np.arange(H)[:, None], runs(n1, H)] + 0.75 * (y[np.arange(H)[:, None], runs(n2, H)]))
    h = mxq(f64(w2), 0, "e4m3").T @ mxq(z, 0, "e4m3")
    st = h - (h[np.arange(N)[:, None], runs(n3, N)])
    return st - (0.5 * (st[np.arange(N)[:, None], runs(n3, N)]))

@@ -1,0 +1,248 @@
+from contextlib import ExitStack
+
+import concourse.mybir as mybir
+
+K, T, S, H, N = 512, 2048, 512, 512, 512
+FLOPS = 2 * K * H * S + 2 * H * N * S
+
+F32 = mybir.dt.float32
+BF16 = mybir.dt.bfloat16
+I32 = mybir.dt.int32
+U32 = mybir.dt.uint32
+U16 = mybir.dt.uint16
+U8 = mybir.dt.uint8
+FP8X4 = mybir.dt.float8_e4m3fn_x4
+COPY = mybir.ActivationFunctionType.Copy
+MULT = mybir.AluOpType.mult
+ADD = mybir.AluOpType.add
+SUB = mybir.AluOpType.subtract
+
+P = 128
+PACK = 4
+HALF = S // 2
+PIECES = ((0, 256), (256, 128), (384, 128))
+W1_VECTOR_SHARE = 80
+
+
+def entries(lists, start, count):
+    return lists[:, start // 16 : (start + count) // 16]
+
+
+def deal_views(grouped, raw, m0, m1):
+    dst = grouped[:].rearrange("p (t m j) -> p m j t", t=PACK, j=PACK)[:, m0:m1]
+    src = raw[:].rearrange("p j (m t) -> p m j t", t=PACK)[:, m0:m1]
+    return dst, src
+
+
+def weave_views(woven, planes):
+    dst = woven[:].rearrange("p (c i t) -> p c t i", i=4, t=PACK)
+    src = planes[:].rearrange("p t (c i) -> p c t i", i=4)
+    return dst, src
+
+
+def tile_picked_hashsumtwice_none_p_kernel(tc, x_words, x_scales, w1, gn, w2, offs, n1, n2, n3, out):
+    nc = tc.nc
+    with ExitStack() as ctx:
+        held = ctx.enter_context(tc.tile_pool(name="held", bufs=1))
+        work = ctx.enter_context(tc.tile_pool(name="work", bufs=1))
+        psum = ctx.enter_context(tc.psum_pool(name="psum", bufs=1))
+
+        offs_sb = held.tile([P, S // 16], U16, name="offs_sb")
+        n1_sb = held.tile([P, S // 16], U16, name="n1_sb")
+        n2_sb = held.tile([P, S // 16], U16, name="n2_sb")
+        n3_sb = held.tile([P, S // 16], U16, name="n3_sb")
+        word_table = held.tile([P, T], U32, name="word_table")
+        byte_table = held.tile([P, T], U8, name="byte_table")
+        gain = held.tile([P, PACK], F32, name="gain")
+        w1_raw = work.tile([P, PACK, H], F32, name="w1_raw", tag="w_raw", align_bytes=64)
+        x_plane = work.tile([P, S], U8, name="x_plane", align_bytes=64)
+
+        nc.gpsimd.memset(byte_table[:].bitcast(I32), 0)
+        nc.gpsimd.memset(x_plane[:].bitcast(I32), 0)
+        nc.scalar.dma_start(gain[:], gn.rearrange("(p t) o -> p (t o)", t=PACK))
+        nc.sync.dma_start(offs_sb[:], offs)
+        nc.scalar.dma_start(byte_table[:].bitcast(I32)[0:P:8, :], x_scales[0].bitcast(I32))
+        nc.sync.dma_start(n3_sb[:], n3)
+        nc.sync.dma_start(w1_raw[:], w1.rearrange("(p j) c -> p j c", j=PACK))
+        nc.sync.dma_start(word_table[:].bitcast(I32), x_words[0].rearrange("p n t -> p (n t)").bitcast(I32))
+        nc.sync.dma_start(n2_sb[:], n2)
+        nc.sync.dma_start(n1_sb[:], n1)
+
+        picked_bytes = work.tile([P, S], U8, name="picked_bytes", align_bytes=64)
+        nc.vector.tensor_copy(picked_bytes[:], byte_table[:].indirect(offs_sb[:]))
+        for q in range(4):
+            nc.scalar.dma_start(
+                x_plane[:].bitcast(I32)[32 * q : 32 * q + 4, :],
+                picked_bytes[:].bitcast(I32)[32 * q : 32 * q + 32 : 8, :],
+            )
+
+        w1_bf = work.tile([P, H * PACK], BF16, name="w1_bf", align_bytes=64)
+        dst, src = deal_views(w1_bf, w1_raw, 0, W1_VECTOR_SHARE)
+        nc.vector.tensor_copy(dst, src)
+        dst, src = deal_views(w1_bf, w1_raw, W1_VECTOR_SHARE, P)
+        nc.scalar.activation(dst, src, COPY)
+        w1_codes = work.tile([P, H], U32, name="w1_codes", align_bytes=64)
+        w1_plane = work.tile([P, H], U8, name="w1_plane", align_bytes=64)
+        nc.vector.quantize_mx(w1_codes[:].bitcast(FP8X4), w1_plane[:], w1_bf[:])
+
+        w2_raw = work.tile([P, PACK, N], F32, name="w2_raw", tag="w_raw", align_bytes=64)
+        nc.sync.dma_start(w2_raw[:], w2.rearrange("(p j) c -> p j c", j=PACK))
+
+        picked_words = []
+        for half in range(2):
+            words = work.tile([P, HALF], U32, name="picked_words%d" % half, align_bytes=64)
+            nc.vector.tensor_copy(words[:], word_table[:].indirect(entries(offs_sb, half * HALF, HALF)))
+            picked_words.append(words)
+
+        y = []
+        for t in range(PACK):
+            rows = slice(t * P, (t + 1) * P)
+            y_t = work.tile([P, S], F32, name="y%d" % t)
+            for half in range(2):
+                cols = slice(half * HALF, (half + 1) * HALF)
+                bank = psum.tile([P, 512], F32, name="y_bank", tag="bank%d" % (2 * t + half))
+                nc.tensor.matmul_mx(
+                    bank[:, 0:HALF],
+                    lhsT=w1_codes[:, rows].bitcast(FP8X4),
+                    lhsT_scale=w1_plane[:, rows],
+                    rhs=picked_words[half][:].bitcast(FP8X4),
+                    rhs_scale=x_plane[:, cols],
+                    start=True,
+                    stop=True,
+                )
+                nc.scalar.activation(y_t[:, cols], bank[:, 0:HALF], COPY, scale=gain[:, t : t + 1])
+            y.append(y_t)
+
+        w2_bf = work.tile([P, N * PACK], BF16, name="w2_bf", tag="w2_bf", align_bytes=64)
+        for quarter in range(4):
+            dst, src = deal_views(w2_bf, w2_raw, 32 * quarter, 32 * (quarter + 1))
+            nc.scalar.activation(dst, src, COPY)
+        w2_codes = work.tile([P, N], U32, name="w2_codes", align_bytes=64)
+        w2_plane = work.tile([P, N], U8, name="w2_plane", align_bytes=64)
+
+        ring = [work.tile([P, HALF], F32, name="ring%d" % r) for r in range(3)]
+        z = [work.tile([P, PACK, width], F32, name="z%d" % a) for a, (start, width) in enumerate(PIECES)]
+        z_bf = [
+            work.tile([P, width * PACK], BF16, name="z_bf%d" % a, tag="z_bf%d" % a if a else "w_raw", align_bytes=64)
+            for a, (start, width) in enumerate(PIECES)
+        ]
+        h_window = [work.tile([P, S], F32, name="h_window%d" % t) for t in range(PACK)]
+        h_plain = work.tile([P, PACK, S], F32, name="h_plain")
+        steps = [(a, t) for a in range(len(PIECES)) for t in range(PACK)]
+        second_term = {}
+
+        def fetch_second(k, tag):
+            a, t = steps[k]
+            start, width = PIECES[a]
+            if tag is None:
+                term = ring[k % 3][:, 0:width]
+            else:
+                fresh = work.tile([P, width], F32, name="term%d" % k, tag=tag, align_bytes=64)
+                term = fresh[:]
+            nc.vector.tensor_scalar(term, y[t][:].indirect(entries(n2_sb, start, width)), 0.75, 0.0, MULT, ADD)
+            second_term[k] = term
+
+        def fetch_first(k):
+            a, t = steps[k]
+            start, width = PIECES[a]
+            nc.vector.tensor_tensor(z[a][:, t, :], y[t][:].indirect(entries(n1_sb, start, width)), second_term[k], ADD)
+
+        def weave(a):
+            dst, src = weave_views(z_bf[a], z[a])
+            if a == len(PIECES) - 1:
+                nc.vector.tensor_copy(dst, src)
+            else:
+                nc.scalar.activation(dst, src, COPY)
+
+        def second_product(a):
+            start, width = PIECES[a]
+            cols = slice(start, start + width)
+            codes = work.tile([P, width], U32, name="z_codes%d" % a, align_bytes=64)
+            plane = work.tile([P, width], U8, name="z_plane%d" % a, align_bytes=64)
+            nc.vector.quantize_mx(codes[:].bitcast(FP8X4), plane[:], z_bf[a][:])
+            per_bank = 1 if a == len(PIECES) - 1 else 2
+            banks = []
+            for b in range(PACK // per_bank):
+                bank = psum.tile([P, 512], F32, name="h_bank", tag="bank%d" % (2 * a + b))
+                for u in range(per_bank):
+                    rows = slice((b * per_bank + u) * P, (b * per_bank + u + 1) * P)
+                    nc.tensor.matmul_mx(
+                        bank[:, u * width : (u + 1) * width],
+                        lhsT=w2_codes[:, rows].bitcast(FP8X4),
+                        lhsT_scale=w2_plane[:, rows],
+                        rhs=codes[:].bitcast(FP8X4),
+                        rhs_scale=plane[:],
+                        start=True,
+                        stop=True,
+                    )
+                banks.append(bank)
+            if per_bank == 1:
+                return banks
+            for b, bank in enumerate(banks):
+                for u in range(per_bank):
+                    nc.scalar.activation(
+                        h_window[b * per_bank + u][:, cols], bank[:, u * width : (u + 1) * width], COPY, scale=0.5
+                    )
+            for b, bank in enumerate(banks):
+                nc.scalar.activation(
+                    h_plain[:, b * per_bank : (b + 1) * per_bank, cols],
+                    bank[:, 0 : per_bank * width].rearrange("p (u c) -> p u c", u=per_bank),
+                    COPY,
+                    scale=0.5,
+                )
+            return banks
+
+        fetch_second(0, None)
+        for k in range(len(steps)):
+            nxt = k + 1
+            if nxt == 5:
+                nc.vector.quantize_mx(w2_codes[:].bitcast(FP8X4), w2_plane[:], w2_bf[:])
+                fetch_second(nxt, "w2_bf")
+            elif nxt == 7:
+                second_product(0)
+                fetch_second(nxt, "w_raw")
+            elif nxt == 11:
+                second_product(1)
+                fetch_second(nxt, "z_bf1")
+            elif nxt < len(steps):
+                fetch_second(nxt, None)
+            fetch_first(k)
+            if steps[k][1] == PACK - 1:
+                weave(steps[k][0])
+        last_banks = second_product(len(PIECES) - 1)
+        last_start, last_width = PIECES[-1]
+        last_cols = slice(last_start, last_start + last_width)
+
+        out_rows = out.rearrange("(p t) j -> p t j", t=PACK)
+        u_window = [work.tile([P, S], F32, name="u_window%d" % t) for t in range(PACK)]
+        st = [work.tile([P, S], F32, name="st%d" % t) for t in range(PACK)]
+
+        def first_hop(t):
+            nc.scalar.activation(h_window[t][:, last_cols], last_banks[t][:, 0:last_width], COPY, scale=0.5)
+            nc.scalar.activation(h_plain[:, t, last_cols], last_banks[t][:, 0:last_width], COPY, scale=0.5)
+            for half in range(2):
+                cols = slice(half * HALF, (half + 1) * HALF)
+                nc.vector.tensor_tensor(
+                    u_window[t][:, cols], h_window[t][:].indirect(entries(n3_sb, half * HALF, HALF)), h_plain[:, t, cols], SUB
+                )
+
+        def second_hop(t):
+            result = work.tile([P, S], F32, name="result%d" % t)
+            for half in range(2):
+                cols = slice(half * HALF, (half + 1) * HALF)
+                nc.scalar.activation(st[t][:, cols], u_window[t][:, cols], COPY, scale=-2.0)
+            for half in range(2):
+                cols = slice(half * HALF, (half + 1) * HALF)
+                nc.vector.tensor_tensor(
+                    result[:, cols], u_window[t][:].indirect(entries(n3_sb, half * HALF, HALF)), st[t][:, cols], ADD
+                )
+                if t == PACK - 1:
+                    nc.sync.dma_start(out_rows[:, t, cols], result[:, cols])
+            if t < PACK - 1:
+                nc.sync.dma_start(out_rows[:, t, :], result[:])
+
+        first_hop(0)
+        for t in range(PACK):
+            if t + 1 < PACK:
+                first_hop(t + 1)
+            second_hop(t)

@@ -20,7 +20,7 @@ SUB = mybir.AluOpType.subtract
 P = 128
 PACK = 4
 HALF = S // 2
-PIECES = ((0, 256), (256, 128), (384, 128))
+WINDOW = 2 * S
 W1_VECTOR_SHARE = 80
 
 
@@ -29,14 +29,14 @@ def entries(lists, start, count):
 
 
 def deal_views(grouped, raw, m0, m1):
-    dst = grouped[:].rearrange("p (t m j) -> p m j t", t=PACK, j=PACK)[:, m0:m1]
-    src = raw[:].rearrange("p j (m t) -> p m j t", t=PACK)[:, m0:m1]
+    dst = grouped.rearrange("p (t m j) -> p m j t", t=PACK, j=PACK)[:, m0:m1]
+    src = raw.rearrange("p (j m t) -> p m j t", j=PACK, t=PACK)[:, m0:m1]
     return dst, src
 
 
 def weave_views(woven, planes):
-    dst = woven[:].rearrange("p (c i t) -> p c t i", i=4, t=PACK)
-    src = planes[:].rearrange("p t (c i) -> p c t i", i=4)
+    dst = woven.rearrange("p (c i t) -> p c t i", i=4, t=PACK)
+    src = planes.rearrange("p (t c i) -> p c t i", i=4, t=PACK)
     return dst, src
 
 
@@ -53,193 +53,164 @@ def tile_picked_hashsumtwice_none_p_kernel(tc, x_words, x_scales, w1, gn, w2, of
         n3_sb = held.tile([P, S // 16], U16, name="n3_sb")
         word_table = held.tile([P, T], U32, name="word_table")
         byte_table = held.tile([P, T], U8, name="byte_table")
-        gain = held.tile([P, PACK], F32, name="gain")
-        w1_raw = work.tile([P, PACK, H], F32, name="w1_raw", tag="w_raw", align_bytes=64)
+        gain = work.tile([P, PACK], F32, name="gain", tag="gain")
         x_plane = work.tile([P, S], U8, name="x_plane", align_bytes=64)
+        staging = work.tile([P, PACK * H], F32, name="staging", align_bytes=64)
+        w_raw = staging[:]
+        z_right = staging[:, 0 : PACK * HALF]
+        z_left_bf = staging[:, 2 * HALF : PACK * HALF].bitcast(BF16)
+        window = [work.tile([P, WINDOW], F32, name="window%d" % t) for t in range(PACK)]
 
-        nc.gpsimd.memset(byte_table[:].bitcast(I32), 0)
-        nc.gpsimd.memset(x_plane[:].bitcast(I32), 0)
-        nc.scalar.dma_start(gain[:], gn.rearrange("(p t) o -> p (t o)", t=PACK))
+        nc.vector.memset(byte_table[:].bitcast(I32), 0)
+        nc.vector.memset(x_plane[:].bitcast(I32), 0)
+        warm = work.tile([P, 1], F32, name="warm")
+        nc.gpsimd.memset(warm[:], 0.0)
+        nc.scalar.activation(warm[:], warm[:], COPY)
+        w1_rows = w1.rearrange("(p j) c -> p (j c)", j=PACK)
+        nc.scalar.dma_start(w_raw[:, 0:H], w1_rows[:, 0:H])
         nc.sync.dma_start(offs_sb[:], offs)
-        nc.scalar.dma_start(byte_table[:].bitcast(I32)[0:P:8, :], x_scales[0].bitcast(I32))
         nc.sync.dma_start(n3_sb[:], n3)
-        nc.sync.dma_start(w1_raw[:], w1.rearrange("(p j) c -> p j c", j=PACK))
-        nc.sync.dma_start(word_table[:].bitcast(I32), x_words[0].rearrange("p n t -> p (n t)").bitcast(I32))
         nc.sync.dma_start(n2_sb[:], n2)
+        nc.sync.dma_start(gain[:], gn.rearrange("(p t) o -> p (t o)", t=PACK))
+        nc.sync.dma_start(byte_table[:].bitcast(I32)[0:P:8, :], x_scales[0].bitcast(I32))
+        nc.sync.dma_start(w_raw[:, H : PACK * H], w1_rows[:, H : PACK * H])
+        nc.sync.dma_start(word_table[:].bitcast(I32), x_words[0].rearrange("p n t -> p (n t)").bitcast(I32))
         nc.sync.dma_start(n1_sb[:], n1)
 
         picked_bytes = work.tile([P, S], U8, name="picked_bytes", align_bytes=64)
         nc.vector.tensor_copy(picked_bytes[:], byte_table[:].indirect(offs_sb[:]))
         for q in range(4):
-            nc.scalar.dma_start(
+            nc.sync.dma_start(
                 x_plane[:].bitcast(I32)[32 * q : 32 * q + 4, :],
                 picked_bytes[:].bitcast(I32)[32 * q : 32 * q + 32 : 8, :],
             )
 
-        w1_bf = work.tile([P, H * PACK], BF16, name="w1_bf", align_bytes=64)
-        dst, src = deal_views(w1_bf, w1_raw, 0, W1_VECTOR_SHARE)
+        w1_bf = work.tile([P, H * PACK], BF16, name="w1_bf", tag="w1_bf", align_bytes=64)
+        dst, src = deal_views(w1_bf[:], w_raw, 0, W1_VECTOR_SHARE)
         nc.vector.tensor_copy(dst, src)
-        dst, src = deal_views(w1_bf, w1_raw, W1_VECTOR_SHARE, P)
-        nc.scalar.activation(dst, src, COPY)
+        dst, src = deal_views(w1_bf[:], w_raw, W1_VECTOR_SHARE, P)
+        nc.scalar.copy(dst, src)
         w1_codes = work.tile([P, H], U32, name="w1_codes", align_bytes=64)
         w1_plane = work.tile([P, H], U8, name="w1_plane", align_bytes=64)
         nc.vector.quantize_mx(w1_codes[:].bitcast(FP8X4), w1_plane[:], w1_bf[:])
 
-        w2_raw = work.tile([P, PACK, N], F32, name="w2_raw", tag="w_raw", align_bytes=64)
-        nc.sync.dma_start(w2_raw[:], w2.rearrange("(p j) c -> p j c", j=PACK))
+        nc.sync.dma_start(w_raw, w2.rearrange("(p j) c -> p (j c)", j=PACK))
 
-        picked_words = []
-        for half in range(2):
-            words = work.tile([P, HALF], U32, name="picked_words%d" % half, align_bytes=64)
-            nc.vector.tensor_copy(words[:], word_table[:].indirect(entries(offs_sb, half * HALF, HALF)))
-            picked_words.append(words)
+        picked_words = work.tile([P, S], U32, name="picked_words", tag="w1_bf", align_bytes=64)
+        halves = [slice(0, HALF), slice(HALF, S)]
+        for cols in halves:
+            nc.vector.tensor_copy(picked_words[:, cols], word_table[:].indirect(entries(offs_sb, cols.start, HALF)))
 
-        y = []
+        def product(bank_no, w_codes, w_plane, codes, plane):
+            width = codes.shape[1]
+            bank = psum.tile([P, 512], F32, name="bank", tag="bank%d" % bank_no)
+            nc.tensor.matmul_mx(
+                bank[:, 0:width],
+                lhsT=w_codes.bitcast(FP8X4),
+                lhsT_scale=w_plane,
+                rhs=codes.bitcast(FP8X4),
+                rhs_scale=plane,
+                start=True,
+                stop=True,
+            )
+            return bank[:, 0:width]
+
         for t in range(PACK):
-            rows = slice(t * P, (t + 1) * P)
-            y_t = work.tile([P, S], F32, name="y%d" % t)
-            for half in range(2):
-                cols = slice(half * HALF, (half + 1) * HALF)
-                bank = psum.tile([P, 512], F32, name="y_bank", tag="bank%d" % (2 * t + half))
-                nc.tensor.matmul_mx(
-                    bank[:, 0:HALF],
-                    lhsT=w1_codes[:, rows].bitcast(FP8X4),
-                    lhsT_scale=w1_plane[:, rows],
-                    rhs=picked_words[half][:].bitcast(FP8X4),
-                    rhs_scale=x_plane[:, cols],
-                    start=True,
-                    stop=True,
-                )
-                nc.scalar.activation(y_t[:, cols], bank[:, 0:HALF], COPY, scale=gain[:, t : t + 1])
-            y.append(y_t)
+            for half, cols in enumerate(halves):
+                rows = slice(t * P, (t + 1) * P)
+                sums = product(2 * t + half, w1_codes[:, rows], w1_plane[:, rows], picked_words[:, cols], x_plane[:, cols])
+                nc.scalar.activation(window[t][:, cols], sums, COPY, scale=gain[:, t : t + 1])
 
-        w2_bf = work.tile([P, N * PACK], BF16, name="w2_bf", tag="w2_bf", align_bytes=64)
+        w2_bf = work.tile([P, N * PACK], BF16, name="w2_bf", align_bytes=64)
         for quarter in range(4):
-            dst, src = deal_views(w2_bf, w2_raw, 32 * quarter, 32 * (quarter + 1))
-            nc.scalar.activation(dst, src, COPY)
-        w2_codes = work.tile([P, N], U32, name="w2_codes", align_bytes=64)
+            dst, src = deal_views(w2_bf[:], w_raw, 32 * quarter, 32 * (quarter + 1))
+            nc.scalar.copy(dst, src)
+        w2_codes_first = work.tile([P, P], U32, name="w2_codes_first", align_bytes=64)
         w2_plane = work.tile([P, N], U8, name="w2_plane", align_bytes=64)
 
-        ring = [work.tile([P, HALF], F32, name="ring%d" % r) for r in range(3)]
-        z = [work.tile([P, PACK, width], F32, name="z%d" % a) for a, (start, width) in enumerate(PIECES)]
-        z_bf = [
-            work.tile([P, width * PACK], BF16, name="z_bf%d" % a, tag="z_bf%d" % a if a else "w_raw", align_bytes=64)
-            for a, (start, width) in enumerate(PIECES)
-        ]
-        h_window = [work.tile([P, S], F32, name="h_window%d" % t) for t in range(PACK)]
-        h_plain = work.tile([P, PACK, S], F32, name="h_plain")
-        steps = [(a, t) for a in range(len(PIECES)) for t in range(PACK)]
-        second_term = {}
+        term = [work.tile([P, S], F32, name="term%d" % t) for t in range(PACK)]
+        for t in range(PACK):
+            nc.vector.tensor_scalar(term[t][:], window[t][:].indirect(n2_sb[:]), 0.75, 0.0, MULT, ADD)
 
-        def fetch_second(k, tag):
-            a, t = steps[k]
-            start, width = PIECES[a]
-            if tag is None:
-                term = ring[k % 3][:, 0:width]
-            else:
-                fresh = work.tile([P, width], F32, name="term%d" % k, tag=tag, align_bytes=64)
-                term = fresh[:]
-            nc.vector.tensor_scalar(term, y[t][:].indirect(entries(n2_sb, start, width)), 0.75, 0.0, MULT, ADD)
-            second_term[k] = term
+        def z_plane(z, t, cols):
+            nc.vector.tensor_tensor(
+                z[:, t * HALF : (t + 1) * HALF], window[t][:].indirect(entries(n1_sb, cols.start, HALF)), term[t][:, cols], ADD
+            )
 
-        def fetch_first(k):
-            a, t = steps[k]
-            start, width = PIECES[a]
-            nc.vector.tensor_tensor(z[a][:, t, :], y[t][:].indirect(entries(n1_sb, start, width)), second_term[k], ADD)
+        z_codes = work.tile([P, S], U32, name="z_codes", align_bytes=64)
+        z_scales = work.tile([P, S], U8, name="z_scales", align_bytes=64)
+        u_window = [work.tile([P, WINDOW], F32, name="u_window%d" % t) for t in range(PACK)]
 
-        def weave(a):
-            dst, src = weave_views(z_bf[a], z[a])
-            if a == len(PIECES) - 1:
-                nc.vector.tensor_copy(dst, src)
-            else:
-                nc.scalar.activation(dst, src, COPY)
+        def first_tile_product(bank_no, cols):
+            return product(bank_no, w2_codes_first[:], w2_plane[:, 0:P], z_codes[:, cols], z_scales[:, cols])
 
-        def second_product(a):
-            start, width = PIECES[a]
-            cols = slice(start, start + width)
-            codes = work.tile([P, width], U32, name="z_codes%d" % a, align_bytes=64)
-            plane = work.tile([P, width], U8, name="z_plane%d" % a, align_bytes=64)
-            nc.vector.quantize_mx(codes[:].bitcast(FP8X4), plane[:], z_bf[a][:])
-            per_bank = 1 if a == len(PIECES) - 1 else 2
-            banks = []
-            for b in range(PACK // per_bank):
-                bank = psum.tile([P, 512], F32, name="h_bank", tag="bank%d" % (2 * a + b))
-                for u in range(per_bank):
-                    rows = slice((b * per_bank + u) * P, (b * per_bank + u + 1) * P)
-                    nc.tensor.matmul_mx(
-                        bank[:, u * width : (u + 1) * width],
-                        lhsT=w2_codes[:, rows].bitcast(FP8X4),
-                        lhsT_scale=w2_plane[:, rows],
-                        rhs=codes[:].bitcast(FP8X4),
-                        rhs_scale=plane[:],
-                        start=True,
-                        stop=True,
-                    )
-                banks.append(bank)
-            if per_bank == 1:
-                return banks
-            for b, bank in enumerate(banks):
-                for u in range(per_bank):
-                    nc.scalar.activation(
-                        h_window[b * per_bank + u][:, cols], bank[:, u * width : (u + 1) * width], COPY, scale=0.5
-                    )
-            for b, bank in enumerate(banks):
-                nc.scalar.activation(
-                    h_plain[:, b * per_bank : (b + 1) * per_bank, cols],
-                    bank[:, 0 : per_bank * width].rearrange("p (u c) -> p u c", u=per_bank),
-                    COPY,
-                    scale=0.5,
-                )
-            return banks
+        def leave_bank(t, cols, sums):
+            nc.scalar.activation(window[t][:, cols], sums, COPY, scale=0.5)
 
-        fetch_second(0, None)
-        for k in range(len(steps)):
-            nxt = k + 1
-            if nxt == 5:
-                nc.vector.quantize_mx(w2_codes[:].bitcast(FP8X4), w2_plane[:], w2_bf[:])
-                fetch_second(nxt, "w2_bf")
-            elif nxt == 7:
-                second_product(0)
-                fetch_second(nxt, "w_raw")
-            elif nxt == 11:
-                second_product(1)
-                fetch_second(nxt, "z_bf1")
-            elif nxt < len(steps):
-                fetch_second(nxt, None)
-            fetch_first(k)
-            if steps[k][1] == PACK - 1:
-                weave(steps[k][0])
-        last_banks = second_product(len(PIECES) - 1)
-        last_start, last_width = PIECES[-1]
-        last_cols = slice(last_start, last_start + last_width)
+        def leave_bank_again(t, cols, sums):
+            nc.scalar.activation(u_window[t][:, S:WINDOW][:, cols], sums, COPY, scale=0.5)
+
+        z_left = work.tile([P, PACK * HALF], F32, name="z_left", tag="gain")
+        for t in range(PACK):
+            z_plane(z_left[:], t, halves[0])
+        dst, src = weave_views(z_left_bf, z_left[:])
+        nc.scalar.copy(dst, src)
+        nc.vector.quantize_mx(w2_codes_first[:].bitcast(FP8X4), w2_plane[:, 0:P], w2_bf[:, 0 : PACK * P])
+        for t in range(2):
+            z_plane(z_right, t, halves[1])
+        nc.vector.quantize_mx(z_codes[:, halves[0]].bitcast(FP8X4), z_scales[:, halves[0]], z_left_bf)
+        sums = first_tile_product(0, halves[0])
+        leave_bank(0, halves[0], sums)
+        leave_bank_again(0, halves[0], sums)
+        for t in range(2, PACK):
+            z_plane(z_right, t, halves[1])
+
+        z_right_bf = work.tile([P, PACK * HALF], BF16, name="z_right_bf", tag="z_right_bf", align_bytes=64)
+        dst, src = weave_views(z_right_bf[:], z_right)
+        nc.vector.tensor_copy(dst[:, 0:32], src[:, 0:32])
+        nc.scalar.copy(dst[:, 32:64], src[:, 32:64])
+        quarters = [slice(HALF, HALF + P), slice(HALF + P, S)]
+        for k, cols in enumerate(quarters):
+            nc.vector.quantize_mx(
+                z_codes[:, cols].bitcast(FP8X4), z_scales[:, cols], z_right_bf[:, k * PACK * P : (k + 1) * PACK * P]
+            )
+        quarter_sums = [first_tile_product(1 + k, cols) for k, cols in enumerate(quarters)]
+        for cols, sums in zip(quarters, quarter_sums):
+            leave_bank(0, cols, sums)
+        for cols, sums in zip(quarters, quarter_sums):
+            leave_bank_again(0, cols, sums)
+
+        w2_codes_rest = work.tile([P, N - P], U32, name="w2_codes_rest", tag="z_right_bf", align_bytes=64)
+        for first, last in ((1, 2), (2, 4)):
+            nc.vector.quantize_mx(
+                w2_codes_rest[:, (first - 1) * P : (last - 1) * P].bitcast(FP8X4),
+                w2_plane[:, first * P : last * P],
+                w2_bf[:, first * PACK * P : last * PACK * P],
+            )
 
         out_rows = out.rearrange("(p t) j -> p t j", t=PACK)
-        u_window = [work.tile([P, S], F32, name="u_window%d" % t) for t in range(PACK)]
-        st = [work.tile([P, S], F32, name="st%d" % t) for t in range(PACK)]
+        whole = slice(0, S)
 
         def first_hop(t):
-            nc.scalar.activation(h_window[t][:, last_cols], last_banks[t][:, 0:last_width], COPY, scale=0.5)
-            nc.scalar.activation(h_plain[:, t, last_cols], last_banks[t][:, 0:last_width], COPY, scale=0.5)
-            for half in range(2):
-                cols = slice(half * HALF, (half + 1) * HALF)
-                nc.vector.tensor_tensor(
-                    u_window[t][:, cols], h_window[t][:].indirect(entries(n3_sb, half * HALF, HALF)), h_plain[:, t, cols], SUB
+            if t > 0:
+                sums = product(
+                    2 + t, w2_codes_rest[:, (t - 1) * P : t * P], w2_plane[:, t * P : (t + 1) * P], z_codes[:], z_scales[:]
                 )
+                leave_bank(t, whole, sums)
+                for cols in halves if t == 1 else [whole]:
+                    leave_bank_again(t, cols, sums[:, cols])
+            for cols in halves if t < 2 else [whole]:
+                looked_up = window[t][:].indirect(entries(n3_sb, cols.start, cols.stop - cols.start))
+                nc.vector.tensor_tensor(u_window[t][:, cols], looked_up, u_window[t][:, S:WINDOW][:, cols], SUB)
 
         def second_hop(t):
+            st = work.tile([P, S], F32, name="st%d" % t)
             result = work.tile([P, S], F32, name="result%d" % t)
-            for half in range(2):
-                cols = slice(half * HALF, (half + 1) * HALF)
-                nc.scalar.activation(st[t][:, cols], u_window[t][:, cols], COPY, scale=-2.0)
-            for half in range(2):
-                cols = slice(half * HALF, (half + 1) * HALF)
-                nc.vector.tensor_tensor(
-                    result[:, cols], u_window[t][:].indirect(entries(n3_sb, half * HALF, HALF)), st[t][:, cols], ADD
-                )
-                if t == PACK - 1:
-                    nc.sync.dma_start(out_rows[:, t, cols], result[:, cols])
-            if t < PACK - 1:
-                nc.sync.dma_start(out_rows[:, t, :], result[:])
+            nc.scalar.activation(st[:], u_window[t][:, 0:S], COPY, scale=-2.0)
+            for cols in halves if t == PACK - 1 else [slice(0, S)]:
+                looked_up = u_window[t][:].indirect(entries(n3_sb, cols.start, cols.stop - cols.start))
+                nc.vector.tensor_tensor(result[:, cols], looked_up, st[:, cols], ADD)
+                nc.sync.dma_start(out_rows[:, t, cols], result[:, cols])
 
         first_hop(0)
         for t in range(PACK):

@@ -58,7 +58,7 @@ def tile_picked_hashsumtwice_none_p_kernel(tc, x_words, x_scales, w1, gn, w2, of
         staging = work.tile([P, PACK * H], F32, name="staging", align_bytes=64)
         w_raw = staging[:]
         z_right = staging[:, 0 : PACK * HALF]
-        z_left_bf = staging[:, 2 * HALF : PACK * HALF].bitcast(BF16)
+        z_left_bf = staging[:, 3 * HALF : 5 * HALF].bitcast(BF16)
         window = [work.tile([P, WINDOW], F32, name="window%d" % t) for t in range(PACK)]
 
         nc.vector.memset(byte_table[:].bitcast(I32), 0)
@@ -67,13 +67,13 @@ def tile_picked_hashsumtwice_none_p_kernel(tc, x_words, x_scales, w1, gn, w2, of
         nc.gpsimd.memset(warm[:], 0.0)
         nc.scalar.activation(warm[:], warm[:], COPY)
         w1_rows = w1.rearrange("(p j) c -> p (j c)", j=PACK)
-        nc.scalar.dma_start(w_raw[:, 0:H], w1_rows[:, 0:H])
+        nc.scalar.dma_start(w_raw[:, 0 : 2 * H], w1_rows[:, 0 : 2 * H])
         nc.sync.dma_start(offs_sb[:], offs)
         nc.sync.dma_start(n3_sb[:], n3)
         nc.sync.dma_start(n2_sb[:], n2)
         nc.sync.dma_start(gain[:], gn.rearrange("(p t) o -> p (t o)", t=PACK))
         nc.sync.dma_start(byte_table[:].bitcast(I32)[0:P:8, :], x_scales[0].bitcast(I32))
-        nc.sync.dma_start(w_raw[:, H : PACK * H], w1_rows[:, H : PACK * H])
+        nc.sync.dma_start(w_raw[:, 2 * H : PACK * H], w1_rows[:, 2 * H : PACK * H])
         nc.sync.dma_start(word_table[:].bitcast(I32), x_words[0].rearrange("p n t -> p (n t)").bitcast(I32))
         nc.sync.dma_start(n1_sb[:], n1)
 
@@ -115,10 +115,13 @@ def tile_picked_hashsumtwice_none_p_kernel(tc, x_words, x_scales, w1, gn, w2, of
             )
             return bank[:, 0:width]
 
+        whole = slice(0, S)
+        quarters = [slice(HALF, HALF + P), slice(HALF + P, S)]
         for t in range(PACK):
-            for half, cols in enumerate(halves):
-                rows = slice(t * P, (t + 1) * P)
-                sums = product(2 * t + half, w1_codes[:, rows], w1_plane[:, rows], picked_words[:, cols], x_plane[:, cols])
+            rows = slice(t * P, (t + 1) * P)
+            for k, cols in enumerate([halves[0]] + quarters if t == 0 else [whole]):
+                bank_no = k if t == 0 else 2 + t
+                sums = product(bank_no, w1_codes[:, rows], w1_plane[:, rows], picked_words[:, cols], x_plane[:, cols])
                 nc.scalar.activation(window[t][:, cols], sums, COPY, scale=gain[:, t : t + 1])
 
         w2_bf = work.tile([P, N * PACK], BF16, name="w2_bf", align_bytes=64)
@@ -128,7 +131,7 @@ def tile_picked_hashsumtwice_none_p_kernel(tc, x_words, x_scales, w1, gn, w2, of
         w2_codes_first = work.tile([P, P], U32, name="w2_codes_first", align_bytes=64)
         w2_plane = work.tile([P, N], U8, name="w2_plane", align_bytes=64)
 
-        term = [work.tile([P, S], F32, name="term%d" % t) for t in range(PACK)]
+        term = [work.tile([P, S], F32, name="term%d" % t, tag="term%d" % t, align_bytes=64) for t in range(PACK)]
         for t in range(PACK):
             nc.vector.tensor_scalar(term[t][:], window[t][:].indirect(n2_sb[:]), 0.75, 0.0, MULT, ADD)
 
@@ -156,20 +159,18 @@ def tile_picked_hashsumtwice_none_p_kernel(tc, x_words, x_scales, w1, gn, w2, of
         dst, src = weave_views(z_left_bf, z_left[:])
         nc.scalar.copy(dst, src)
         nc.vector.quantize_mx(w2_codes_first[:].bitcast(FP8X4), w2_plane[:, 0:P], w2_bf[:, 0 : PACK * P])
-        for t in range(2):
+        for t in range(PACK - 1):
             z_plane(z_right, t, halves[1])
         nc.vector.quantize_mx(z_codes[:, halves[0]].bitcast(FP8X4), z_scales[:, halves[0]], z_left_bf)
         sums = first_tile_product(0, halves[0])
         leave_bank(0, halves[0], sums)
-        leave_bank_again(0, halves[0], sums)
-        for t in range(2, PACK):
-            z_plane(z_right, t, halves[1])
+        z_plane(z_right, PACK - 1, halves[1])
 
-        z_right_bf = work.tile([P, PACK * HALF], BF16, name="z_right_bf", tag="z_right_bf", align_bytes=64)
+        z_right_bf = work.tile([P, PACK * HALF], BF16, name="z_right_bf", align_bytes=64)
         dst, src = weave_views(z_right_bf[:], z_right)
         nc.vector.tensor_copy(dst[:, 0:32], src[:, 0:32])
         nc.scalar.copy(dst[:, 32:64], src[:, 32:64])
-        quarters = [slice(HALF, HALF + P), slice(HALF + P, S)]
+        leave_bank_again(0, halves[0], sums)
         for k, cols in enumerate(quarters):
             nc.vector.quantize_mx(
                 z_codes[:, cols].bitcast(FP8X4), z_scales[:, cols], z_right_bf[:, k * PACK * P : (k + 1) * PACK * P]
@@ -180,7 +181,7 @@ def tile_picked_hashsumtwice_none_p_kernel(tc, x_words, x_scales, w1, gn, w2, of
         for cols, sums in zip(quarters, quarter_sums):
             leave_bank_again(0, cols, sums)
 
-        w2_codes_rest = work.tile([P, N - P], U32, name="w2_codes_rest", tag="z_right_bf", align_bytes=64)
+        w2_codes_rest = work.tile([P, N - P], U32, name="w2_codes_rest", tag="term%d" % (PACK - 1), align_bytes=64)
         for first, last in ((1, 2), (2, 4)):
             nc.vector.quantize_mx(
                 w2_codes_rest[:, (first - 1) * P : (last - 1) * P].bitcast(FP8X4),
@@ -189,7 +190,6 @@ def tile_picked_hashsumtwice_none_p_kernel(tc, x_words, x_scales, w1, gn, w2, of
             )
 
         out_rows = out.rearrange("(p t) j -> p t j", t=PACK)
-        whole = slice(0, S)
 
         def first_hop(t):
             if t > 0:

from contextlib import ExitStack

import concourse.mybir as mybir

K, T, S, H, N = 512, 2048, 512, 512, 512
FLOPS = 2 * K * H * S + 2 * H * N * S

F32 = mybir.dt.float32
BF16 = mybir.dt.bfloat16
I32 = mybir.dt.int32
U32 = mybir.dt.uint32
U16 = mybir.dt.uint16
U8 = mybir.dt.uint8
FP8X4 = mybir.dt.float8_e4m3fn_x4
COPY = mybir.ActivationFunctionType.Copy
MULT = mybir.AluOpType.mult
ADD = mybir.AluOpType.add
SUB = mybir.AluOpType.subtract

P = 128
PACK = 4
HALF = S // 2
WINDOW = 2 * S
W1_VECTOR_SHARE = 80


def entries(lists, start, count):
    return lists[:, start // 16 : (start + count) // 16]


def deal_views(grouped, raw, m0, m1):
    dst = grouped.rearrange("p (t m j) -> p m j t", t=PACK, j=PACK)[:, m0:m1]
    src = raw.rearrange("p (j m t) -> p m j t", j=PACK, t=PACK)[:, m0:m1]
    return dst, src


def weave_views(woven, planes):
    dst = woven.rearrange("p (c i t) -> p c t i", i=4, t=PACK)
    src = planes.rearrange("p (t c i) -> p c t i", i=4, t=PACK)
    return dst, src


def tile_picked_hashsumtwice_none_p_kernel(tc, x_words, x_scales, w1, gn, w2, offs, n1, n2, n3, out):
    nc = tc.nc
    with ExitStack() as ctx:
        held = ctx.enter_context(tc.tile_pool(name="held", bufs=1))
        work = ctx.enter_context(tc.tile_pool(name="work", bufs=1))
        psum = ctx.enter_context(tc.psum_pool(name="psum", bufs=1))

        offs_sb = held.tile([P, S // 16], U16, name="offs_sb")
        n1_sb = held.tile([P, S // 16], U16, name="n1_sb")
        n2_sb = held.tile([P, S // 16], U16, name="n2_sb")
        n3_sb = held.tile([P, S // 16], U16, name="n3_sb")
        word_table = held.tile([P, T], U32, name="word_table")
        byte_table = held.tile([P, T], U8, name="byte_table")
        gain = work.tile([P, PACK], F32, name="gain", tag="gain")
        x_plane = work.tile([P, S], U8, name="x_plane", align_bytes=64)
        staging = work.tile([P, PACK * H], F32, name="staging", align_bytes=64)
        w_raw = staging[:]
        z_right = staging[:, 0 : PACK * HALF]
        z_left_bf = staging[:, 3 * HALF : 5 * HALF].bitcast(BF16)
        window = [work.tile([P, WINDOW], F32, name="window%d" % t) for t in range(PACK)]

        nc.vector.memset(byte_table[:].bitcast(I32), 0)
        nc.vector.memset(x_plane[:].bitcast(I32), 0)
        warm = work.tile([P, 1], F32, name="warm")
        nc.gpsimd.memset(warm[:], 0.0)
        nc.scalar.activation(warm[:], warm[:], COPY)
        w1_rows = w1.rearrange("(p j) c -> p (j c)", j=PACK)
        nc.scalar.dma_start(w_raw[:, 0 : 2 * H], w1_rows[:, 0 : 2 * H])
        nc.sync.dma_start(offs_sb[:], offs)
        nc.sync.dma_start(n3_sb[:], n3)
        nc.sync.dma_start(n2_sb[:], n2)
        nc.sync.dma_start(gain[:], gn.rearrange("(p t) o -> p (t o)", t=PACK))
        nc.sync.dma_start(byte_table[:].bitcast(I32)[0:P:8, :], x_scales[0].bitcast(I32))
        nc.sync.dma_start(w_raw[:, 2 * H : PACK * H], w1_rows[:, 2 * H : PACK * H])
        nc.sync.dma_start(word_table[:].bitcast(I32), x_words[0].rearrange("p n t -> p (n t)").bitcast(I32))
        nc.sync.dma_start(n1_sb[:], n1)

        picked_bytes = work.tile([P, S], U8, name="picked_bytes", align_bytes=64)
        nc.vector.tensor_copy(picked_bytes[:], byte_table[:].indirect(offs_sb[:]))
        for q in range(4):
            nc.sync.dma_start(
                x_plane[:].bitcast(I32)[32 * q : 32 * q + 4, :],
                picked_bytes[:].bitcast(I32)[32 * q : 32 * q + 32 : 8, :],
            )

        w1_bf = work.tile([P, H * PACK], BF16, name="w1_bf", tag="w1_bf", align_bytes=64)
        dst, src = deal_views(w1_bf[:], w_raw, 0, W1_VECTOR_SHARE)
        nc.vector.tensor_copy(dst, src)
        dst, src = deal_views(w1_bf[:], w_raw, W1_VECTOR_SHARE, P)
        nc.scalar.copy(dst, src)
        w1_codes = work.tile([P, H], U32, name="w1_codes", align_bytes=64)
        w1_plane = work.tile([P, H], U8, name="w1_plane", align_bytes=64)
        nc.vector.quantize_mx(w1_codes[:].bitcast(FP8X4), w1_plane[:], w1_bf[:])

        nc.sync.dma_start(w_raw, w2.rearrange("(p j) c -> p (j c)", j=PACK))

        picked_words = work.tile([P, S], U32, name="picked_words", tag="w1_bf", align_bytes=64)
        halves = [slice(0, HALF), slice(HALF, S)]
        for cols in halves:
            nc.vector.tensor_copy(picked_words[:, cols], word_table[:].indirect(entries(offs_sb, cols.start, HALF)))

        def product(bank_no, w_codes, w_plane, codes, plane):
            width = codes.shape[1]
            bank = psum.tile([P, 512], F32, name="bank", tag="bank%d" % bank_no)
            nc.tensor.matmul_mx(
                bank[:, 0:width],
                lhsT=w_codes.bitcast(FP8X4),
                lhsT_scale=w_plane,
                rhs=codes.bitcast(FP8X4),
                rhs_scale=plane,
                start=True,
                stop=True,
            )
            return bank[:, 0:width]

        whole = slice(0, S)
        quarters = [slice(HALF, HALF + P), slice(HALF + P, S)]
        for t in range(PACK):
            rows = slice(t * P, (t + 1) * P)
            for k, cols in enumerate([halves[0]] + quarters if t == 0 else [whole]):
                bank_no = k if t == 0 else 2 + t
                sums = product(bank_no, w1_codes[:, rows], w1_plane[:, rows], picked_words[:, cols], x_plane[:, cols])
                nc.scalar.activation(window[t][:, cols], sums, COPY, scale=gain[:, t : t + 1])

        w2_bf = work.tile([P, N * PACK], BF16, name="w2_bf", align_bytes=64)
        for quarter in range(4):
            dst, src = deal_views(w2_bf[:], w_raw, 32 * quarter, 32 * (quarter + 1))
            nc.scalar.copy(dst, src)
        w2_codes_first = work.tile([P, P], U32, name="w2_codes_first", align_bytes=64)
        w2_plane = work.tile([P, N], U8, name="w2_plane", align_bytes=64)

        term = [work.tile([P, S], F32, name="term%d" % t, tag="term%d" % t, align_bytes=64) for t in range(PACK)]
        for t in range(PACK):
            nc.vector.tensor_scalar(term[t][:], window[t][:].indirect(n2_sb[:]), 0.75, 0.0, MULT, ADD)

        def z_plane(z, t, cols):
            nc.vector.tensor_tensor(
                z[:, t * HALF : (t + 1) * HALF], window[t][:].indirect(entries(n1_sb, cols.start, HALF)), term[t][:, cols], ADD
            )

        z_codes = work.tile([P, S], U32, name="z_codes", align_bytes=64)
        z_scales = work.tile([P, S], U8, name="z_scales", align_bytes=64)
        u_window = [work.tile([P, WINDOW], F32, name="u_window%d" % t) for t in range(PACK)]

        def first_tile_product(bank_no, cols):
            return product(bank_no, w2_codes_first[:], w2_plane[:, 0:P], z_codes[:, cols], z_scales[:, cols])

        def leave_bank(t, cols, sums):
            nc.scalar.activation(window[t][:, cols], sums, COPY, scale=0.5)

        def leave_bank_again(t, cols, sums):
            nc.scalar.activation(u_window[t][:, S:WINDOW][:, cols], sums, COPY, scale=0.5)

        z_left = work.tile([P, PACK * HALF], F32, name="z_left", tag="gain")
        for t in range(PACK):
            z_plane(z_left[:], t, halves[0])
        dst, src = weave_views(z_left_bf, z_left[:])
        nc.scalar.copy(dst, src)
        nc.vector.quantize_mx(w2_codes_first[:].bitcast(FP8X4), w2_plane[:, 0:P], w2_bf[:, 0 : PACK * P])
        for t in range(PACK - 1):
            z_plane(z_right, t, halves[1])
        nc.vector.quantize_mx(z_codes[:, halves[0]].bitcast(FP8X4), z_scales[:, halves[0]], z_left_bf)
        sums = first_tile_product(0, halves[0])
        leave_bank(0, halves[0], sums)
        z_plane(z_right, PACK - 1, halves[1])

        z_right_bf = work.tile([P, PACK * HALF], BF16, name="z_right_bf", align_bytes=64)
        dst, src = weave_views(z_right_bf[:], z_right)
        nc.vector.tensor_copy(dst[:, 0:32], src[:, 0:32])
        nc.scalar.copy(dst[:, 32:64], src[:, 32:64])
        leave_bank_again(0, halves[0], sums)
        for k, cols in enumerate(quarters):
            nc.vector.quantize_mx(
                z_codes[:, cols].bitcast(FP8X4), z_scales[:, cols], z_right_bf[:, k * PACK * P : (k + 1) * PACK * P]
            )
        quarter_sums = [first_tile_product(1 + k, cols) for k, cols in enumerate(quarters)]
        for cols, sums in zip(quarters, quarter_sums):
            leave_bank(0, cols, sums)
        for cols, sums in zip(quarters, quarter_sums):
            leave_bank_again(0, cols, sums)

        w2_codes_rest = work.tile([P, N - P], U32, name="w2_codes_rest", tag="term%d" % (PACK - 1), align_bytes=64)
        for first, last in ((1, 2), (2, 4)):
            nc.vector.quantize_mx(
                w2_codes_rest[:, (first - 1) * P : (last - 1) * P].bitcast(FP8X4),
                w2_plane[:, first * P : last * P],
                w2_bf[:, first * PACK * P : last * PACK * P],
            )

        out_rows = out.rearrange("(p t) j -> p t j", t=PACK)

        def first_hop(t):
            if t > 0:
                sums = product(
                    2 + t, w2_codes_rest[:, (t - 1) * P : t * P], w2_plane[:, t * P : (t + 1) * P], z_codes[:], z_scales[:]
                )
                leave_bank(t, whole, sums)
                for cols in halves if t == 1 else [whole]:
                    leave_bank_again(t, cols, sums[:, cols])
            for cols in halves if t < 2 else [whole]:
                looked_up = window[t][:].indirect(entries(n3_sb, cols.start, cols.stop - cols.start))
                nc.vector.tensor_tensor(u_window[t][:, cols], looked_up, u_window[t][:, S:WINDOW][:, cols], SUB)

        def second_hop(t):
            st = work.tile([P, S], F32, name="st%d" % t)
            result = work.tile([P, S], F32, name="result%d" % t)
            nc.scalar.activation(st[:], u_window[t][:, 0:S], COPY, scale=-2.0)
            for cols in halves if t == PACK - 1 else [slice(0, S)]:
                looked_up = u_window[t][:].indirect(entries(n3_sb, cols.start, cols.stop - cols.start))
                nc.vector.tensor_tensor(result[:, cols], looked_up, st[:, cols], ADD)
                nc.sync.dma_start(out_rows[:, t, cols], result[:, cols])

        first_hop(0)
        for t in range(PACK):
            if t + 1 < PACK:
                first_hop(t + 1)
            second_hop(t)
